import numpy as np
import ml_dtypes


def mxq(x, axis, fmt="e4m3"):
    dtype, down = {"e4m3": (ml_dtypes.float8_e4m3fn, 7), "e5m2": (ml_dtypes.float8_e5m2, 14)}[fmt]
    v = np.moveaxis(np.asarray(x, np.float32).astype(ml_dtypes.bfloat16).astype(np.float64), axis, -1)
    blocks = v.reshape(v.shape[:-1] + (-1, 32))
    amax = np.abs(blocks).max(-1, keepdims=True)
    byte = np.maximum(np.where(amax > 0, np.frexp(amax)[1] - 1 + 127, 0) - down, 1)
    scale = np.exp2(byte - 127.0)
    codes = (blocks / scale).astype(np.float32).astype(dtype).astype(np.float64)
    return np.moveaxis((codes * scale).reshape(v.shape), -1, axis)


WIDE = False


def mx_kscale(k):
    if not WIDE:
        return np.ones(k)
    levels = np.array([10, -10, 5, -5, 0])
    if k % 512:
        return np.exp2(np.random.permutation(np.resize(levels, k // 32))).repeat(32)
    a = np.empty((k // 512, 16))
    for p in range(k // 512):
        a[p, :8] = np.random.permutation(np.resize(levels, 8))
        for g in range(8):
            far = levels[np.abs(levels - a[p, g]) >= 10]
            a[p, g + 8] = far[np.random.randint(len(far))]
    return np.exp2(a.ravel()).repeat(32)


def f64(x):
    return np.asarray(x).astype(np.float64)


def striped(idx):
    return np.tile(idx.reshape(-1, 16).T, (8, 1)).astype(np.uint16)


def unstriped(offs):
    return offs[:16].T.reshape(-1).astype(np.int64)


E2M1 = np.array([0.0, 0.5, 1.0, 1.5, 2.0, 3.0, 4.0, 6.0, -0.0, -0.5, -1.0, -1.5, -2.0, -3.0, -4.0, -6.0])


def pack_weight(w, fmt):
    k, n = w.shape
    w = f64(np.asarray(w, np.float32).astype(ml_dtypes.bfloat16)).reshape(k // 32, 32, n)
    amax = np.abs(w).max(1)
    if fmt == "e4m3":
        byte = np.frexp(amax)[1] - 1 + 127 - 7
    else:
        mant, ex = np.frexp(amax / 6.0)
        byte = np.where(mant > 0.5, ex, ex - 1) + 127
    byte = np.clip(np.where(amax > 0, byte, 1), 1, 254)
    scaled = (w * np.exp2(127.0 - byte)[:, None, :]).reshape(k, n).astype(np.float32)
    by_word = np.ascontiguousarray(scaled.reshape(k // 512, 128, 4, n).transpose(0, 1, 3, 2))
    if fmt == "e4m3":
        words = by_word.astype(ml_dtypes.float8_e4m3fn).view(np.uint8)
    else:
        c = by_word.astype(ml_dtypes.float4_e2m1fn).view(np.uint8) & 0xF
        words = (c[..., 0::2] | (c[..., 1::2] << 4)).reshape(k // 512, 128, 2 * n)
    return np.ascontiguousarray(words), np.ascontiguousarray(byte.astype(np.uint8).reshape(k // 512, 16, n))


def unpack_weight(words, scales, fmt):
    g, _, n = scales.shape
    words = np.ascontiguousarray(words).reshape(g, 128, n, -1)
    if fmt == "e4m3":
        vals = words.view(ml_dtypes.float8_e4m3fn).astype(np.float64)
    else:
        nib = np.empty((g, 128, n, 4), np.uint8)
        nib[..., 0::2] = words & 0xF
        nib[..., 1::2] = words >> 4
        vals = E2M1[nib]
    vals = vals * np.repeat(np.exp2(scales.astype(np.float64) - 127.0), 8, axis=1)[..., None]
    return vals.transpose(0, 1, 3, 2).reshape(g * 512, n)


def gelu(v):
    return 0.5 * v * (1.0 + np.tanh(np.sqrt(2.0 / np.pi) * (v + 0.044715 * v**3)))


def striped8(idx):
    return np.concatenate([v.reshape(-1, 16).T for v in idx]).astype(np.uint16)


def unstriped8(offs):
    return np.stack([offs[16 * g:16 * g + 16].T.reshape(-1) for g in range(8)]).astype(np.int64)


def heads(h, wgt, idx8):
    r = np.arange(h.shape[0])
    return wgt[r // 4 % 128] * h[r[:, None], idx8[r % 512 // 64]]


def bf(x):
    return np.asarray(x, np.float32).astype(ml_dtypes.bfloat16)


def planes(Y):
    n, m = Y.shape
    b = f64(bf(Y)).reshape(n // 32, 32, m)
    amax = np.abs(b).max(1)
    byte = np.clip(np.where(amax > 0, np.frexp(amax)[1] - 1 + 127 - 7, 1), 1, 254)
    codes = (b * np.exp2(127.0 - byte)[:, None, :]).reshape(n, m).astype(np.float32).astype(ml_dtypes.float8_e4m3fn).view(np.uint8)
    words = codes.reshape(n // 512, 128, 4, m).transpose(0, 1, 3, 2)
    return np.ascontiguousarray(words), np.ascontiguousarray(byte.astype(np.uint8).reshape(n // 512, 16, m))


K, T, H, S, T2, P, N = 1536, 2048, 1024, 512, 1024, 512, 512

def setup_inputs():
    n = np.random.standard_normal
    s = mx_kscale(K)[:, None]
    u = mx_kscale(H)[:, None]
    tab_words, tab_scales = pack_weight(n((K, T)) * s, "e4m3")
    w4 = n((H, N)) / np.sqrt(H) * np.exp(0.8 * n(N)) / u
    w4_words, w4_scales = pack_weight(w4, "e2m1")
    legs = np.stack([np.random.permutation(T2)[:P] for _ in range(8)])
    return {
        "tab_words": tab_words, "tab_scales": tab_scales,
        "offs": striped(np.random.permutation(T)[:S]),
        "w1": (1.5 * n((K, H)) / np.sqrt(K) / s).astype(np.float32),
        "b1": (0.6 * n(H)).astype(np.float32),
        "gain": (1.5 * np.exp(0.3 * n(H)) * u[:, 0]).astype(np.float32),
        "page0": (n((H, T2)) * u).astype(np.float32),
        "wgs": np.exp(0.3 * n((128, S))).astype(np.float32),
        "offs2": striped(np.random.permutation(T2)[:S]),
        "wgt": np.repeat(np.random.uniform(0.5, 2.0, (8, P)), 16, axis=0).astype(np.float32),
        "offs3": striped8(legs),
        "gm": n((H, P)).astype(np.float32),
        "gv": (n(H) * u[:, 0]).astype(np.float32),
        "w4_words": w4_words, "w4_scales": w4_scales,
    }

def reference(tab_words, tab_scales, offs, w1, b1, gain, page0, wgs, offs2, wgt, offs3, gm, gv, w4_words, w4_scales):
    v = unpack_weight(tab_words, tab_scales, "e4m3")[:, unstriped(offs)]
    w4 = unpack_weight(w4_words, w4_scales, "e2m1")
    d = (mxq(f64(w1), 0, "e4m3").T @ v) + f64(b1)[:, None]
    h = f64(gain)[:, None] * np.tanh(d)
    page = f64(page0).copy()
    page[:, unstriped(offs2)] = np.tile(f64(wgs), (H // 128, 1)) * h
    x = heads(page, f64(wgt), unstriped8(offs3))
    z = np.maximum(x * f64(gm), x + f64(gv)[:, None])
    y = w4.T @ mxq(z, 0, "e4m3")
    words, scales = planes(y)
    return y, words, scales

@@ -1,0 +1,323 @@
+from contextlib import ExitStack
+
+import concourse.mybir as mybir
+from concourse.masks import make_identity
+
+K, T, H, S, T2, PICKS, N = 1536, 2048, 1024, 512, 1024, 512, 512
+FLOPS = 2 * K * H * S + 2 * H * N * PICKS
+
+F32 = mybir.dt.float32
+BF16 = mybir.dt.bfloat16
+I32 = mybir.dt.int32
+U32 = mybir.dt.uint32
+U16 = mybir.dt.uint16
+U8 = mybir.dt.uint8
+FP8X4 = mybir.dt.float8_e4m3fn_x4
+FP4X4 = mybir.dt.float4_e2m1fn_x4
+ALU = mybir.AluOpType
+ACT = mybir.ActivationFunctionType
+
+P = 128
+PACK = 4
+GROUP = P * PACK
+K_PASSES = K // GROUP
+H_PASSES = H // GROUP
+TILES = H // P
+CHUNK = 128
+CHUNKS = PICKS // CHUNK
+QUADS = 4
+
+
+def tile_list_motion_cue_features_kernel(
+    tc, tab_words, tab_scales, offs, w1, b1, gain, page0, wgs, offs2, wgt, offs3, gm, gv,
+    w4_words, w4_scales, out_0, out_1, out_2,
+):
+    nc = tc.nc
+    with ExitStack() as ctx:
+        lists = ctx.enter_context(tc.tile_pool(name="lists", bufs=1))
+        keep = ctx.enter_context(tc.tile_pool(name="keep", bufs=1))
+        ring = ctx.enter_context(tc.tile_pool(name="ring", bufs=2))
+        h_psum = ctx.enter_context(tc.psum_pool(name="h_psum", bufs=4))
+        aux_psum = ctx.enter_context(tc.psum_pool(name="aux_psum", bufs=4))
+
+        def load_list(source, name):
+            tile = lists.tile([P, 32], U16, name=name)
+            nc.sync.dma_start(tile[:], source)
+            return tile
+
+        def load_vector(source, name):
+            tile = keep.tile([P, H_PASSES, PACK], F32, name=name)
+            nc.sync.dma_start(tile[:], source.rearrange("(b p i) -> p b i", b=H_PASSES, i=PACK))
+            return tile
+
+        def column(vector, t):
+            return vector[:, t // PACK, t % PACK : t % PACK + 1]
+
+        tab_sc = keep.tile([P, T], U8, name="tab_sc", align_bytes=64)
+        w4_sc_raw = keep.tile([P, H_PASSES, N], U8, name="w4_sc_raw", align_bytes=64)
+        nc.vector.memset(tab_sc[:].bitcast(I32), 0)
+        nc.vector.memset(w4_sc_raw[:].bitcast(I32), 0)
+        ident = keep.tile([P, P], F32, name="ident")
+        make_identity(nc, ident[:])
+
+        def load_tab_scales():
+            for q in range(QUADS):
+                nc.sync.dma_start(
+                    tab_sc[32 * q : 32 * q + 4 * K_PASSES, :].bitcast(I32),
+                    tab_scales[:, 4 * q : 4 * q + 4, :].bitcast(I32),
+                )
+
+        def load_w4_scales():
+            for q in range(QUADS):
+                nc.sync.dma_start(
+                    w4_sc_raw[32 * q : 32 * q + 4, :, :].bitcast(I32),
+                    w4_scales[:, 4 * q : 4 * q + 4, :].rearrange("a r n -> r a n").bitcast(I32),
+                )
+
+        def load_w1(a, b):
+            tile = keep.tile([P, PACK, GROUP], F32, name=f"w1_raw{a}{b}", tag="w1_raw", bufs=K_PASSES)
+            rows = w1[a * GROUP : (a + 1) * GROUP, b * GROUP : (b + 1) * GROUP]
+            nc.sync.dma_start(tile[:], rows.rearrange("(p j) c -> p j c", j=PACK))
+            return tile
+
+        def load_tab(a):
+            tile = keep.tile([P, T], I32, name=f"tab{a}")
+            nc.sync.dma_start(tile[:], tab_words[a].rearrange("p n i -> p (n i)").bitcast(I32))
+            return tile
+
+        def dealt_rows(source, t):
+            b, i = divmod(t, PACK)
+            return source[b * GROUP : (b + 1) * GROUP, :].rearrange("(p i) c -> p i c", i=PACK)[:, i, :]
+
+        pages = {}
+        gm_sb = keep.tile([P, TILES, PICKS], F32, name="gm_sb")
+
+        def load_page(t):
+            pages[t] = keep.tile([P, T2], F32, name=f"page{t}")
+            nc.sync.dma_start(pages[t][:], dealt_rows(page0, t))
+
+        def load_gm(t):
+            nc.sync.dma_start(gm_sb[:, t, :], dealt_rows(gm, t))
+
+        w1_raw, tab = {}, {}
+        w1_raw[0, 0] = load_w1(0, 0)
+        idx = load_list(offs, "idx")
+        wgs_sb = keep.tile([P, S], F32, name="wgs_sb")
+        nc.sync.dma_start(wgs_sb[:], wgs)
+        w4_raw = keep.tile([P, H_PASSES, 2 * N], U8, name="w4_raw", align_bytes=64)
+        nc.sync.dma_start(w4_raw[:].bitcast(I32), w4_words.rearrange("a p n -> p a n").bitcast(I32))
+        gain_sb = load_vector(gain, "gain_sb")
+        b1_sb = load_vector(b1, "b1_sb")
+        idx2 = load_list(offs2, "idx2")
+        tab[0] = load_tab(0)
+        load_tab_scales()
+        w1_raw[1, 0] = load_w1(1, 0)
+        tab[1] = load_tab(1)
+        w1_raw[2, 0] = load_w1(2, 0)
+        tab[2] = load_tab(2)
+        load_w4_scales()
+        load_page(0)
+        idx3 = load_list(offs3, "idx3")
+        gv_sb = load_vector(gv, "gv_sb")
+        load_page(1)
+        wgt_sb = keep.tile([P, PICKS], F32, name="wgt_sb")
+        nc.sync.dma_start(wgt_sb[:], wgt)
+        load_gm(0)
+        load_page(2)
+        load_page(3)
+        load_gm(1)
+        w1_raw[0, 1] = load_w1(0, 1)
+        w1_raw[1, 1] = load_w1(1, 1)
+        load_gm(2)
+        load_page(4)
+        w1_raw[2, 1] = load_w1(2, 1)
+        load_gm(3)
+        for t in range(5, TILES):
+            load_page(t)
+        for t in range(4, TILES):
+            load_gm(t)
+
+        wgs_t_ps = aux_psum.tile([P, S // P, P], F32, name="wgs_t_ps", tag="aux")
+        for c in range(S // P):
+            nc.tensor.transpose(wgs_t_ps[:, c, :], wgs_sb[:, c * P : (c + 1) * P], ident[:])
+        wgs_t = keep.tile([P, S // P, PACK, QUADS, 32], F32, name="wgs_t")
+        nc.scalar.copy(
+            wgs_t[:].rearrange("j c i r p -> j c r p i"),
+            wgs_t_ps[:].rearrange("j c (p i) -> j c p i", i=PACK).unsqueeze(2).broadcast_to([P, S // P, QUADS, 32, PACK]),
+        )
+        wz = keep.tile([P, TILES + 2, S], F32, name="wz")
+        dealt_ps = []
+        for i in range(PACK):
+            bank = aux_psum.tile([P, S], F32, name=f"dealt{i}", tag="aux")
+            for c in range(S // P):
+                nc.tensor.transpose(bank[:, c * P : (c + 1) * P], wgs_t[:, c, i, :, :].rearrange("j r p -> j (r p)"), ident[:])
+            dealt_ps.append(bank)
+
+        def scale_wgs(t):
+            nc.scalar.activation(wz[:, t, :], dealt_ps[t % PACK][:], ACT.Copy, scale=column(gain_sb, t))
+
+        w1_codes, w1_sc = {}, {}
+
+        def quantize_w1(a, b, shares):
+            grouped = ring.tile([P, PACK, P, PACK], BF16, name="w1_bf", align_bytes=64)
+            for cast, m0, m1 in shares:
+                cast(
+                    grouped[:].rearrange("p t m j -> p m j t")[:, m0:m1],
+                    w1_raw[a, b][:].rearrange("p j (m t) -> p m j t", t=PACK)[:, m0:m1],
+                )
+            w1_codes[a, b] = keep.tile([P, GROUP], U32, name=f"w1_codes{a}{b}", align_bytes=64)
+            w1_sc[a, b] = keep.tile([P, GROUP], U8, name=f"w1_sc{a}{b}", align_bytes=64)
+            nc.vector.quantize_mx(
+                out=w1_codes[a, b][:].bitcast(FP8X4), scales=w1_sc[a, b][:],
+                in_=grouped[:].rearrange("p t m j -> p (t m j)"),
+            )
+
+        v_codes = {}
+
+        def gather_tab(a):
+            v_codes[a] = keep.tile([P, S], U32, name=f"v_codes{a}", align_bytes=64)
+            nc.vector.tensor_copy(v_codes[a][:], tab[a][:].bitcast(U32).indirect(idx[:]))
+
+        v_sc = keep.tile([P, S], U8, name="v_sc", align_bytes=64)
+        h_banks = {}
+
+        def first_pass(a, b):
+            for i in range(PACK):
+                t = PACK * b + i
+                if a == 0:
+                    h_banks[t] = h_psum.tile([P, S], F32, name=f"h{t}", tag="h")
+                cols = slice(i * P, (i + 1) * P)
+                nc.tensor.matmul_mx(
+                    out=h_banks[t][:],
+                    lhsT=w1_codes[a, b][:, cols].bitcast(FP8X4), lhsT_scale=w1_sc[a, b][:, cols],
+                    rhs=v_codes[a][:].bitcast(FP8X4), rhs_scale=v_sc[4 * a :, :],
+                    start=(a == 0), stop=(a == K_PASSES - 1),
+                )
+
+        hx = keep.tile([P, TILES + 1, S], F32, name="hx")
+
+        def tanh(t):
+            nc.scalar.activation(hx[:, t, :], h_banks[t][:], ACT.Tanh, bias=column(b1_sb, t))
+
+        w4_codes = keep.tile([P, H_PASSES, PACK, 2 * P], U8, name="w4_codes", align_bytes=64)
+        nc.vector.tensor_copy(
+            w4_codes[:].bitcast(U16).rearrange("p a t m -> p a m t"),
+            w4_raw[:].bitcast(U16).rearrange("p a (m t) -> p a m t", t=PACK),
+        )
+        quantize_w1(0, 0, [(nc.scalar.copy, 0, P)])
+        gather_tab(0)
+        nc.vector.tensor_copy(v_sc[:], tab_sc[:].indirect(idx[:]))
+        first_pass(0, 0)
+        scale_wgs(0)
+        quantize_w1(1, 0, [(nc.scalar.copy, 0, P)])
+        gather_tab(1)
+        first_pass(1, 0)
+        scale_wgs(1)
+
+        quantize_w1(2, 0, [(nc.vector.tensor_copy, 0, 80), (nc.scalar.copy, 80, P)])
+        gather_tab(2)
+        first_pass(2, 0)
+        w4_sc = keep.tile([P, H_PASSES, PACK, P], U8, name="w4_sc", align_bytes=64)
+        nc.vector.tensor_copy(
+            w4_sc[:].rearrange("p a t m -> p a m t"),
+            w4_sc_raw[:].rearrange("p a (m t) -> p a m t", t=PACK),
+        )
+
+        for t in range(PACK):
+            tanh(t)
+        for t in range(2, TILES):
+            scale_wgs(t)
+
+        def scatter(t):
+            nc.vector.tensor_tensor(pages[t][:].indirect(idx2[:]), hx[:, t, :], wz[:, t, :], ALU.mult)
+
+        def gather(t, m0, m1):
+            nc.vector.tensor_tensor(
+                hx[:, t + 1, m0:m1], pages[t][:].indirect(idx3[:, m0 // 16 : m1 // 16]), wgt_sb[:, m0:m1], ALU.mult
+            )
+
+        def modulate(t0, t1, m0, m1):
+            product = ring.tile([P, t1 - t0, m1 - m0], F32, name="product")
+            nc.vector.tensor_tensor(product[:], hx[:, t0 + 1 : t1 + 1, m0:m1], gm_sb[:, t0:t1, m0:m1], ALU.mult)
+            return product
+
+        def larger(t, product, m0, m1):
+            nc.vector.scalar_tensor_tensor(
+                wz[:, t + 2, m0:m1], hx[:, t + 1, m0:m1], column(gv_sb, t), product, ALU.add, ALU.max
+            )
+
+        def quantize_z(b, m0, m1, cast):
+            width = m1 - m0
+            grouped = keep.tile([P, width, PACK], BF16, name=f"z_bf{b}_{m0}", align_bytes=64)
+            cast(
+                grouped[:].rearrange("p (c e) i -> p c i e", e=4),
+                wz[:, PACK * b + 2 : PACK * b + 6, m0:m1].rearrange("p i (c e) -> p c i e", e=4),
+            )
+            codes = keep.tile([P, width], U32, name=f"z_codes{b}_{m0}", align_bytes=64)
+            scales = keep.tile([P, width], U8, name=f"z_sc{b}_{m0}", align_bytes=64)
+            nc.vector.quantize_mx(out=codes[:].bitcast(FP8X4), scales=scales[:], in_=grouped[:].rearrange("p m i -> p (m i)"))
+            return codes, scales
+
+        y_banks = {}
+
+        def second_pass(b, q, codes, scales):
+            if b == 0:
+                y_banks[q] = aux_psum.tile([P, PACK, CHUNK], F32, name=f"y{q}", tag="aux")
+            for t in range(PACK):
+                nc.tensor.matmul_mx(
+                    out=y_banks[q][:, t, :],
+                    lhsT=w4_codes[:, b, t, :].bitcast(FP4X4),
+                    lhsT_scale=w4_sc[:, b, t, :],
+                    rhs=codes.bitcast(FP8X4), rhs_scale=scales,
+                    start=(b == 0 and t == 0), stop=(b == H_PASSES - 1 and t == PACK - 1),
+                )
+
+        products = {}
+        scatter(0)
+        for t in range(TILES - 1):
+            scatter(t + 1)
+            if t >= 1:
+                products[t - 1] = modulate(t - 1, t, 0, PICKS)
+            if t < TILES - 2:
+                gather(t, 0, PICKS)
+            if t >= 1:
+                larger(t - 1, products[t - 1][:, 0, :], 0, PICKS)
+            if t < K_PASSES:
+                quantize_w1(t, 1, [(nc.scalar.copy, 0, P)])
+                first_pass(t, 1)
+            if t == K_PASSES - 1:
+                for later in range(PACK, TILES):
+                    tanh(later)
+            if t == PACK:
+                codes, scales = quantize_z(0, 0, PICKS, nc.scalar.copy)
+                for q in range(CHUNKS):
+                    cols = slice(q * CHUNK, (q + 1) * CHUNK)
+                    second_pass(0, q, codes[:, cols], scales[:, cols])
+
+        y_rows = out_0.rearrange("(p t) m -> p t m", t=PACK)
+        y_words = out_1[0].rearrange("p m t -> p (m t)").bitcast(I32)
+        y_codes = keep.tile([P, PICKS], U32, name="y_codes", align_bytes=64)
+        y_sc = keep.tile([P, PICKS], U8, name="y_sc", align_bytes=64)
+        for q in range(CHUNKS):
+            m0, m1 = q * CHUNK, (q + 1) * CHUNK
+            last = q == CHUNKS - 1
+            cast = nc.vector.tensor_copy if last else nc.scalar.copy
+            gather(TILES - 2, m0, m1)
+            gather(TILES - 1, m0, m1)
+            product = modulate(TILES - 2, TILES, m0, m1)
+            larger(TILES - 2, product[:, 0, :], m0, m1)
+            larger(TILES - 1, product[:, 1, :], m0, m1)
+            codes, scales = quantize_z(1, m0, m1, cast)
+            second_pass(1, q, codes[:], scales[:])
+            y_bf = keep.tile([P, CHUNK, PACK], BF16, name=f"y_bf{q}", align_bytes=64)
+            cast(y_bf[:], y_banks[q][:].rearrange("p t m -> p m t"))
+            y_sb = keep.tile([P, PACK, CHUNK], F32, name=f"y_sb{q}")
+            nc.scalar.copy(y_sb[:], y_banks[q][:])
+            nc.vector.quantize_mx(
+                out=y_codes[:, m0:m1].bitcast(FP8X4), scales=y_sc[:, m0:m1], in_=y_bf[:].rearrange("p m t -> p (m t)")
+            )
+            (nc.scalar if last else nc.sync).dma_start(y_rows[:, :, m0:m1], y_sb[:])
+            nc.sync.dma_start(y_words[:, m0:m1], y_codes[:, m0:m1].bitcast(I32))
+        for q in range(QUADS):
+            queue = nc.sync if q < 2 else nc.scalar
+            queue.dma_start(out_2[0, 4 * q : 4 * q + 4, :].bitcast(I32), y_sc[32 * q : 32 * q + 4, :].bitcast(I32))

@@ -104,8 +104,6 @@ def tile_list_motion_cue_features_kernel(
         idx = load_list(offs, "idx")
         wgs_sb = keep.tile([P, S], F32, name="wgs_sb")
         nc.sync.dma_start(wgs_sb[:], wgs)
-        w4_raw = keep.tile([P, H_PASSES, 2 * N], U8, name="w4_raw", align_bytes=64)
-        nc.sync.dma_start(w4_raw[:].bitcast(I32), w4_words.rearrange("a p n -> p a n").bitcast(I32))
         gain_sb = load_vector(gain, "gain_sb")
         b1_sb = load_vector(b1, "b1_sb")
         idx2 = load_list(offs2, "idx2")
@@ -115,6 +113,8 @@ def tile_list_motion_cue_features_kernel(
         tab[1] = load_tab(1)
         w1_raw[2, 0] = load_w1(2, 0)
         tab[2] = load_tab(2)
+        w4_raw = keep.tile([P, H_PASSES, 2 * N], U8, name="w4_raw", align_bytes=64)
+        nc.sync.dma_start(w4_raw[:].bitcast(I32), w4_words.rearrange("a p n -> p a n").bitcast(I32))
         load_w4_scales()
         load_page(0)
         idx3 = load_list(offs3, "idx3")
@@ -123,19 +123,15 @@ def tile_list_motion_cue_features_kernel(
         wgt_sb = keep.tile([P, PICKS], F32, name="wgt_sb")
         nc.sync.dma_start(wgt_sb[:], wgt)
         load_gm(0)
-        load_page(2)
-        load_page(3)
-        load_gm(1)
         w1_raw[0, 1] = load_w1(0, 1)
         w1_raw[1, 1] = load_w1(1, 1)
-        load_gm(2)
-        load_page(4)
+        load_page(2)
+        load_gm(1)
         w1_raw[2, 1] = load_w1(2, 1)
-        load_gm(3)
-        for t in range(5, TILES):
+        for t in range(3, TILES):
             load_page(t)
-        for t in range(4, TILES):
-            load_gm(t)
+            load_gm(t - 1)
+        load_gm(TILES - 1)
 
         wgs_t_ps = aux_psum.tile([P, S // P, P], F32, name="wgs_t_ps", tag="aux")
         for c in range(S // P):
@@ -199,11 +195,6 @@ def tile_list_motion_cue_features_kernel(
         def tanh(t):
             nc.scalar.activation(hx[:, t, :], h_banks[t][:], ACT.Tanh, bias=column(b1_sb, t))
 
-        w4_codes = keep.tile([P, H_PASSES, PACK, 2 * P], U8, name="w4_codes", align_bytes=64)
-        nc.vector.tensor_copy(
-            w4_codes[:].bitcast(U16).rearrange("p a t m -> p a m t"),
-            w4_raw[:].bitcast(U16).rearrange("p a (m t) -> p a m t", t=PACK),
-        )
         quantize_w1(0, 0, [(nc.scalar.copy, 0, P)])
         gather_tab(0)
         nc.vector.tensor_copy(v_sc[:], tab_sc[:].indirect(idx[:]))
@@ -217,6 +208,11 @@ def tile_list_motion_cue_features_kernel(
         quantize_w1(2, 0, [(nc.vector.tensor_copy, 0, 80), (nc.scalar.copy, 80, P)])
         gather_tab(2)
         first_pass(2, 0)
+        w4_codes = keep.tile([P, H_PASSES, PACK, 2 * P], U8, name="w4_codes", align_bytes=64)
+        nc.vector.tensor_copy(
+            w4_codes[:].bitcast(U16).rearrange("p a t m -> p a m t"),
+            w4_raw[:].bitcast(U16).rearrange("p a (m t) -> p a m t", t=PACK),
+        )
         w4_sc = keep.tile([P, H_PASSES, PACK, P], U8, name="w4_sc", align_bytes=64)
         nc.vector.tensor_copy(
             w4_sc[:].rearrange("p a t m -> p a m t"),
@@ -231,19 +227,22 @@ def tile_list_motion_cue_features_kernel(
         def scatter(t):
             nc.vector.tensor_tensor(pages[t][:].indirect(idx2[:]), hx[:, t, :], wz[:, t, :], ALU.mult)
 
+        def picked(t):
+            return w1_raw[t, 1][:, 0, :] if t < K_PASSES else hx[:, t + 1, :]
+
         def gather(t, m0, m1):
             nc.vector.tensor_tensor(
-                hx[:, t + 1, m0:m1], pages[t][:].indirect(idx3[:, m0 // 16 : m1 // 16]), wgt_sb[:, m0:m1], ALU.mult
+                picked(t)[:, m0:m1], pages[t][:].indirect(idx3[:, m0 // 16 : m1 // 16]), wgt_sb[:, m0:m1], ALU.mult
             )
 
-        def modulate(t0, t1, m0, m1):
-            product = ring.tile([P, t1 - t0, m1 - m0], F32, name="product")
-            nc.vector.tensor_tensor(product[:], hx[:, t0 + 1 : t1 + 1, m0:m1], gm_sb[:, t0:t1, m0:m1], ALU.mult)
+        def modulate(x, factors):
+            product = ring.tile(list(x.shape), F32, name="product")
+            nc.vector.tensor_tensor(product[:], x, factors, ALU.mult)
             return product
 
         def larger(t, product, m0, m1):
             nc.vector.scalar_tensor_tensor(
-                wz[:, t + 2, m0:m1], hx[:, t + 1, m0:m1], column(gv_sb, t), product, ALU.add, ALU.max
+                wz[:, t + 2, m0:m1], picked(t)[:, m0:m1], column(gv_sb, t), product, ALU.add, ALU.max
             )
 
         def quantize_z(b, m0, m1, cast):
@@ -277,14 +276,14 @@ def tile_list_motion_cue_features_kernel(
         for t in range(TILES - 1):
             scatter(t + 1)
             if t >= 1:
-                products[t - 1] = modulate(t - 1, t, 0, PICKS)
-            if t < TILES - 2:
-                gather(t, 0, PICKS)
-            if t >= 1:
-                larger(t - 1, products[t - 1][:, 0, :], 0, PICKS)
+                products[t - 1] = modulate(picked(t - 1), gm_sb[:, t - 1, :])
             if t < K_PASSES:
                 quantize_w1(t, 1, [(nc.scalar.copy, 0, P)])
                 first_pass(t, 1)
+            if t < TILES - 2:
+                gather(t, 0, PICKS)
+            if t >= 1:
+                larger(t - 1, products[t - 1][:], 0, PICKS)
             if t == K_PASSES - 1:
                 for later in range(PACK, TILES):
                     tanh(later)
@@ -304,7 +303,7 @@ def tile_list_motion_cue_features_kernel(
             cast = nc.vector.tensor_copy if last else nc.scalar.copy
             gather(TILES - 2, m0, m1)
             gather(TILES - 1, m0, m1)
-            product = modulate(TILES - 2, TILES, m0, m1)
+            product = modulate(hx[:, TILES - 1 :, m0:m1], gm_sb[:, TILES - 2 :, m0:m1])
             larger(TILES - 2, product[:, 0, :], m0, m1)
             larger(TILES - 1, product[:, 1, :], m0, m1)
             codes, scales = quantize_z(1, m0, m1, cast)

@@ -90,7 +90,7 @@ def tile_list_motion_cue_features_kernel(
             return source[b * GROUP : (b + 1) * GROUP, :].rearrange("(p i) c -> p i c", i=PACK)[:, i, :]
 
         pages = {}
-        gm_sb = keep.tile([P, TILES, PICKS], F32, name="gm_sb")
+        gm_sb = keep.tile([P, TILES + 1, PICKS], F32, name="gm_sb")
 
         def load_page(t):
             pages[t] = keep.tile([P, T2], F32, name=f"page{t}")
@@ -122,13 +122,17 @@ def tile_list_motion_cue_features_kernel(
         load_page(1)
         wgt_sb = keep.tile([P, PICKS], F32, name="wgt_sb")
         nc.sync.dma_start(wgt_sb[:], wgt)
-        load_gm(0)
         w1_raw[0, 1] = load_w1(0, 1)
         w1_raw[1, 1] = load_w1(1, 1)
         load_page(2)
-        load_gm(1)
+        load_gm(0)
         w1_raw[2, 1] = load_w1(2, 1)
-        for t in range(3, TILES):
+        load_gm(2)
+        load_page(4)
+        load_gm(3)
+        load_page(3)
+        load_gm(1)
+        for t in range(5, TILES):
             load_page(t)
             load_gm(t - 1)
         load_gm(TILES - 1)
@@ -190,7 +194,7 @@ def tile_list_motion_cue_features_kernel(
                     start=(a == 0), stop=(a == K_PASSES - 1),
                 )
 
-        hx = keep.tile([P, TILES + 1, S], F32, name="hx")
+        hx = keep.tile([P, TILES, S], F32, name="hx")
 
         def tanh(t):
             nc.scalar.activation(hx[:, t, :], h_banks[t][:], ACT.Tanh, bias=column(b1_sb, t))
@@ -224,20 +228,32 @@ def tile_list_motion_cue_features_kernel(
         for t in range(2, TILES):
             scale_wgs(t)
 
+        placed_first = keep.tile([P, PACK, S], F32, name="placed_first")
+
+        def placed(t):
+            return placed_first[:, t, :] if t < PACK else gm_sb[:, t - 3, :]
+
+        def weigh(t, engine):
+            engine.tensor_tensor(placed(t), hx[:, t, :], wz[:, t, :], ALU.mult)
+
         def scatter(t):
-            nc.vector.tensor_tensor(pages[t][:].indirect(idx2[:]), hx[:, t, :], wz[:, t, :], ALU.mult)
+            nc.vector.tensor_copy(pages[t][:].indirect(idx2[:]), placed(t))
 
         def picked(t):
-            return w1_raw[t, 1][:, 0, :] if t < K_PASSES else hx[:, t + 1, :]
+            if t < 2:
+                return w1_raw[t, 1][:, 0, :]
+            if t < TILES - 2:
+                return hx[:, t + 2, :]
+            return gm_sb[:, 5 + 3 * (t - TILES + 2), :]
 
         def gather(t, m0, m1):
             nc.vector.tensor_tensor(
                 picked(t)[:, m0:m1], pages[t][:].indirect(idx3[:, m0 // 16 : m1 // 16]), wgt_sb[:, m0:m1], ALU.mult
             )
 
-        def modulate(x, factors):
+        def modulate(x, factors, engine):
             product = ring.tile(list(x.shape), F32, name="product")
-            nc.vector.tensor_tensor(product[:], x, factors, ALU.mult)
+            engine.tensor_tensor(product[:], x, factors, ALU.mult)
             return product
 
         def larger(t, product, m0, m1):
@@ -271,23 +287,33 @@ def tile_list_motion_cue_features_kernel(
                     start=(b == 0 and t == 0), stop=(b == H_PASSES - 1 and t == PACK - 1),
                 )
 
+        def second_half_pass(a):
+            quantize_w1(a, 1, [(nc.scalar.copy, 0, P)])
+            first_pass(a, 1)
+
         products = {}
+        weigh(0, nc.vector)
+        for t in range(1, PACK):
+            weigh(t, nc.gpsimd)
         scatter(0)
-        for t in range(TILES - 1):
-            scatter(t + 1)
-            if t >= 1:
-                products[t - 1] = modulate(picked(t - 1), gm_sb[:, t - 1, :])
-            if t < K_PASSES:
-                quantize_w1(t, 1, [(nc.scalar.copy, 0, P)])
-                first_pass(t, 1)
-            if t < TILES - 2:
-                gather(t, 0, PICKS)
-            if t >= 1:
-                larger(t - 1, products[t - 1][:], 0, PICKS)
-            if t == K_PASSES - 1:
+        scatter(1)
+        second_half_pass(0)
+        gather(0, 0, PICKS)
+        for t in range(TILES - 2):
+            scatter(t + 2)
+            products[t] = modulate(picked(t), gm_sb[:, t, :], nc.gpsimd)
+            if t == 0:
+                second_half_pass(1)
+            if PACK <= t + 3 < TILES:
+                weigh(t + 3, nc.gpsimd)
+            larger(t, products[t][:], 0, PICKS)
+            if t + 1 < TILES - 2:
+                gather(t + 1, 0, PICKS)
+            if t == 0:
+                second_half_pass(2)
                 for later in range(PACK, TILES):
                     tanh(later)
-            if t == PACK:
+            if t == PACK - 1:
                 codes, scales = quantize_z(0, 0, PICKS, nc.scalar.copy)
                 for q in range(CHUNKS):
                     cols = slice(q * CHUNK, (q + 1) * CHUNK)
@@ -303,7 +329,7 @@ def tile_list_motion_cue_features_kernel(
             cast = nc.vector.tensor_copy if last else nc.scalar.copy
             gather(TILES - 2, m0, m1)
             gather(TILES - 1, m0, m1)
-            product = modulate(hx[:, TILES - 1 :, m0:m1], gm_sb[:, TILES - 2 :, m0:m1])
+            product = modulate(gm_sb[:, 5 : TILES + 1 : 3, m0:m1], gm_sb[:, TILES - 2 : TILES, m0:m1], nc.vector)
             larger(TILES - 2, product[:, 0, :], m0, m1)
             larger(TILES - 1, product[:, 1, :], m0, m1)
             codes, scales = quantize_z(1, m0, m1, cast)

@@ -90,7 +90,7 @@ def tile_list_motion_cue_features_kernel(
             return source[b * GROUP : (b + 1) * GROUP, :].rearrange("(p i) c -> p i c", i=PACK)[:, i, :]
 
         pages = {}
-        gm_sb = keep.tile([P, TILES + 1, PICKS], F32, name="gm_sb")
+        gm_sb = keep.tile([P, TILES, PICKS], F32, name="gm_sb")
 
         def load_page(t):
             pages[t] = keep.tile([P, T2], F32, name=f"page{t}")
@@ -105,34 +105,30 @@ def tile_list_motion_cue_features_kernel(
         wgs_sb = keep.tile([P, S], F32, name="wgs_sb")
         nc.sync.dma_start(wgs_sb[:], wgs)
         gain_sb = load_vector(gain, "gain_sb")
+        tab[0] = load_tab(0)
+        w1_raw[1, 0] = load_w1(1, 0)
         b1_sb = load_vector(b1, "b1_sb")
         idx2 = load_list(offs2, "idx2")
-        tab[0] = load_tab(0)
         load_tab_scales()
-        w1_raw[1, 0] = load_w1(1, 0)
         tab[1] = load_tab(1)
         w1_raw[2, 0] = load_w1(2, 0)
+        load_w4_scales()
         tab[2] = load_tab(2)
         w4_raw = keep.tile([P, H_PASSES, 2 * N], U8, name="w4_raw", align_bytes=64)
         nc.sync.dma_start(w4_raw[:].bitcast(I32), w4_words.rearrange("a p n -> p a n").bitcast(I32))
-        load_w4_scales()
         load_page(0)
         idx3 = load_list(offs3, "idx3")
         gv_sb = load_vector(gv, "gv_sb")
         load_page(1)
         wgt_sb = keep.tile([P, PICKS], F32, name="wgt_sb")
         nc.sync.dma_start(wgt_sb[:], wgt)
+        load_gm(0)
         w1_raw[0, 1] = load_w1(0, 1)
         w1_raw[1, 1] = load_w1(1, 1)
         load_page(2)
-        load_gm(0)
-        w1_raw[2, 1] = load_w1(2, 1)
-        load_gm(2)
-        load_page(4)
-        load_gm(3)
-        load_page(3)
         load_gm(1)
-        for t in range(5, TILES):
+        w1_raw[2, 1] = load_w1(2, 1)
+        for t in range(3, TILES):
             load_page(t)
             load_gm(t - 1)
         load_gm(TILES - 1)
@@ -194,7 +190,7 @@ def tile_list_motion_cue_features_kernel(
                     start=(a == 0), stop=(a == K_PASSES - 1),
                 )
 
-        hx = keep.tile([P, TILES, S], F32, name="hx")
+        hx = keep.tile([P, TILES + 1, S], F32, name="hx")
 
         def tanh(t):
             nc.scalar.activation(hx[:, t, :], h_banks[t][:], ACT.Tanh, bias=column(b1_sb, t))
@@ -210,6 +206,11 @@ def tile_list_motion_cue_features_kernel(
         scale_wgs(1)
 
         quantize_w1(2, 0, [(nc.vector.tensor_copy, 0, 80), (nc.scalar.copy, 80, P)])
+        w4_sc = keep.tile([P, H_PASSES, PACK, P], U8, name="w4_sc", align_bytes=64)
+        nc.vector.tensor_copy(
+            w4_sc[:].rearrange("p a t m -> p a m t"),
+            w4_sc_raw[:].rearrange("p a (m t) -> p a m t", t=PACK),
+        )
         gather_tab(2)
         first_pass(2, 0)
         w4_codes = keep.tile([P, H_PASSES, PACK, 2 * P], U8, name="w4_codes", align_bytes=64)
@@ -217,43 +218,26 @@ def tile_list_motion_cue_features_kernel(
             w4_codes[:].bitcast(U16).rearrange("p a t m -> p a m t"),
             w4_raw[:].bitcast(U16).rearrange("p a (m t) -> p a m t", t=PACK),
         )
-        w4_sc = keep.tile([P, H_PASSES, PACK, P], U8, name="w4_sc", align_bytes=64)
-        nc.vector.tensor_copy(
-            w4_sc[:].rearrange("p a t m -> p a m t"),
-            w4_sc_raw[:].rearrange("p a (m t) -> p a m t", t=PACK),
-        )
 
         for t in range(PACK):
             tanh(t)
         for t in range(2, TILES):
             scale_wgs(t)
 
-        placed_first = keep.tile([P, PACK, S], F32, name="placed_first")
-
-        def placed(t):
-            return placed_first[:, t, :] if t < PACK else gm_sb[:, t - 3, :]
-
-        def weigh(t, engine):
-            engine.tensor_tensor(placed(t), hx[:, t, :], wz[:, t, :], ALU.mult)
-
         def scatter(t):
-            nc.vector.tensor_copy(pages[t][:].indirect(idx2[:]), placed(t))
+            nc.vector.tensor_tensor(pages[t][:].indirect(idx2[:]), hx[:, t, :], wz[:, t, :], ALU.mult)
 
         def picked(t):
-            if t < 2:
-                return w1_raw[t, 1][:, 0, :]
-            if t < TILES - 2:
-                return hx[:, t + 2, :]
-            return gm_sb[:, 5 + 3 * (t - TILES + 2), :]
+            return w1_raw[t, 1][:, 0, :] if t < K_PASSES else hx[:, t + 1, :]
 
         def gather(t, m0, m1):
             nc.vector.tensor_tensor(
                 picked(t)[:, m0:m1], pages[t][:].indirect(idx3[:, m0 // 16 : m1 // 16]), wgt_sb[:, m0:m1], ALU.mult
             )
 
-        def modulate(x, factors, engine):
-            product = ring.tile(list(x.shape), F32, name="product")
-            engine.tensor_tensor(product[:], x, factors, ALU.mult)
+        def modulate(x, factors):
+            product = ring.tile(list(x.shape), F32, name="product", bufs=3)
+            nc.vector.tensor_tensor(product[:], x, factors, ALU.mult)
             return product
 
         def larger(t, product, m0, m1):
@@ -276,44 +260,36 @@ def tile_list_motion_cue_features_kernel(
         y_banks = {}
 
         def second_pass(b, q, codes, scales):
-            if b == 0:
-                y_banks[q] = aux_psum.tile([P, PACK, CHUNK], F32, name=f"y{q}", tag="aux")
+            per_bank = 2 if q == CHUNKS - 1 else PACK
             for t in range(PACK):
+                first, place = t - t % per_bank, t % per_bank
+                if b == 0 and place == 0:
+                    pool, tag = (h_psum, "h") if per_bank < PACK else (aux_psum, "aux")
+                    y_banks[q, first] = pool.tile([P, per_bank, CHUNK], F32, name=f"y{q}_{first}", tag=tag)
                 nc.tensor.matmul_mx(
-                    out=y_banks[q][:, t, :],
+                    out=y_banks[q, first][:, place, :],
                     lhsT=w4_codes[:, b, t, :].bitcast(FP4X4),
                     lhsT_scale=w4_sc[:, b, t, :],
                     rhs=codes.bitcast(FP8X4), rhs_scale=scales,
-                    start=(b == 0 and t == 0), stop=(b == H_PASSES - 1 and t == PACK - 1),
+                    start=(b == 0 and place == 0), stop=(b == H_PASSES - 1 and place == per_bank - 1),
                 )
 
-        def second_half_pass(a):
-            quantize_w1(a, 1, [(nc.scalar.copy, 0, P)])
-            first_pass(a, 1)
-
         products = {}
-        weigh(0, nc.vector)
-        for t in range(1, PACK):
-            weigh(t, nc.gpsimd)
         scatter(0)
-        scatter(1)
-        second_half_pass(0)
-        gather(0, 0, PICKS)
-        for t in range(TILES - 2):
-            scatter(t + 2)
-            products[t] = modulate(picked(t), gm_sb[:, t, :], nc.gpsimd)
-            if t == 0:
-                second_half_pass(1)
-            if PACK <= t + 3 < TILES:
-                weigh(t + 3, nc.gpsimd)
-            larger(t, products[t][:], 0, PICKS)
-            if t + 1 < TILES - 2:
-                gather(t + 1, 0, PICKS)
-            if t == 0:
-                second_half_pass(2)
+        for t in range(TILES - 1):
+            scatter(t + 1)
+            if t >= 1:
+                products[t - 1] = modulate(picked(t - 1), gm_sb[:, t - 1, :])
+            if t < K_PASSES:
+                quantize_w1(t, 1, [(nc.scalar.copy, 0, P)])
+                first_pass(t, 1)
+            gather(t, 0, PICKS)
+            if t >= 1:
+                larger(t - 1, products[t - 1][:], 0, PICKS)
+            if t == K_PASSES - 1:
                 for later in range(PACK, TILES):
                     tanh(later)
-            if t == PACK - 1:
+            if t == PACK:
                 codes, scales = quantize_z(0, 0, PICKS, nc.scalar.copy)
                 for q in range(CHUNKS):
                     cols = slice(q * CHUNK, (q + 1) * CHUNK)
@@ -326,23 +302,35 @@ def tile_list_motion_cue_features_kernel(
         for q in range(CHUNKS):
             m0, m1 = q * CHUNK, (q + 1) * CHUNK
             last = q == CHUNKS - 1
-            cast = nc.vector.tensor_copy if last else nc.scalar.copy
-            gather(TILES - 2, m0, m1)
             gather(TILES - 1, m0, m1)
-            product = modulate(gm_sb[:, 5 : TILES + 1 : 3, m0:m1], gm_sb[:, TILES - 2 : TILES, m0:m1], nc.vector)
-            larger(TILES - 2, product[:, 0, :], m0, m1)
-            larger(TILES - 1, product[:, 1, :], m0, m1)
-            codes, scales = quantize_z(1, m0, m1, cast)
+            if q < 2:
+                upto = m1 if q == 0 else PICKS
+                product = modulate(picked(TILES - 2)[:, m0:upto], gm_sb[:, TILES - 2, m0:upto])
+                larger(TILES - 2, product[:], m0, upto)
+            product = modulate(picked(TILES - 1)[:, m0:m1], gm_sb[:, TILES - 1, m0:m1])
+            larger(TILES - 1, product[:], m0, m1)
+            codes, scales = quantize_z(1, m0, m1, nc.scalar.copy if q == 0 else nc.vector.tensor_copy)
             second_pass(1, q, codes[:], scales[:])
             y_bf = keep.tile([P, CHUNK, PACK], BF16, name=f"y_bf{q}", align_bytes=64)
-            cast(y_bf[:], y_banks[q][:].rearrange("p t m -> p m t"))
             y_sb = keep.tile([P, PACK, CHUNK], F32, name=f"y_sb{q}")
-            nc.scalar.copy(y_sb[:], y_banks[q][:])
+            if q == 0:
+                nc.scalar.copy(y_bf[:], y_banks[q, 0][:].rearrange("p t m -> p m t"))
+            if last:
+                nc.scalar.copy(y_sb[:, 0:2, :], y_banks[q, 0][:])
+                nc.vector.tensor_copy(y_sb[:, 2:4, :], y_banks[q, 2][:])
+            else:
+                nc.scalar.copy(y_sb[:], y_banks[q, 0][:])
+            if q > 0:
+                nc.vector.tensor_copy(
+                    y_bf[:].rearrange("p (c e) t -> p c t e", e=4), y_sb[:].rearrange("p t (c e) -> p c t e", e=4)
+                )
             nc.vector.quantize_mx(
                 out=y_codes[:, m0:m1].bitcast(FP8X4), scales=y_sc[:, m0:m1], in_=y_bf[:].rearrange("p m t -> p (m t)")
             )
             (nc.scalar if last else nc.sync).dma_start(y_rows[:, :, m0:m1], y_sb[:])
-            nc.sync.dma_start(y_words[:, m0:m1], y_codes[:, m0:m1].bitcast(I32))
+            if q >= CHUNKS - 2:
+                stored = m0 if last else 0
+                nc.sync.dma_start(y_words[:, stored:m1], y_codes[:, stored:m1].bitcast(I32))
         for q in range(QUADS):
             queue = nc.sync if q < 2 else nc.scalar
             queue.dma_start(out_2[0, 4 * q : 4 * q + 4, :].bitcast(I32), y_sc[32 * q : 32 * q + 4, :].bitcast(I32))

@@ -23,9 +23,14 @@ GROUP = P * PACK
 K_PASSES = K // GROUP
 H_PASSES = H // GROUP
 TILES = H // P
+LIST = 16
+QUADS = 4
+SCALE_ROWS = 4
+RUN = 4
 CHUNK = 128
 CHUNKS = PICKS // CHUNK
-QUADS = 4
+VECTOR_SHARE = 80
+H_BANKS, AUX_BANKS = 4, 4
 
 
 def tile_list_motion_cue_features_kernel(
@@ -37,11 +42,18 @@ def tile_list_motion_cue_features_kernel(
         lists = ctx.enter_context(tc.tile_pool(name="lists", bufs=1))
         keep = ctx.enter_context(tc.tile_pool(name="keep", bufs=1))
         ring = ctx.enter_context(tc.tile_pool(name="ring", bufs=2))
-        h_psum = ctx.enter_context(tc.psum_pool(name="h_psum", bufs=4))
-        aux_psum = ctx.enter_context(tc.psum_pool(name="aux_psum", bufs=4))
+        h_psum = ctx.enter_context(tc.psum_pool(name="h_psum", bufs=H_BANKS))
+        aux_psum = ctx.enter_context(tc.psum_pool(name="aux_psum", bufs=AUX_BANKS))
+
+        tab_sc = keep.tile([P, T], U8, name="tab_sc", align_bytes=64)
+        w4_sc_raw = keep.tile([P, H_PASSES, N], U8, name="w4_sc_raw", align_bytes=64)
+        nc.vector.memset(tab_sc[:].bitcast(I32), 0)
+        nc.vector.memset(w4_sc_raw[:].bitcast(I32), 0)
+        ident = keep.tile([P, P], F32, name="ident")
+        make_identity(nc, ident[:])
 
         def load_list(source, name):
-            tile = lists.tile([P, 32], U16, name=name)
+            tile = lists.tile([P, S // LIST], U16, name=name)
             nc.sync.dma_start(tile[:], source)
             return tile
 
@@ -53,43 +65,36 @@ def tile_list_motion_cue_features_kernel(
         def column(vector, t):
             return vector[:, t // PACK, t % PACK : t % PACK + 1]
 
-        tab_sc = keep.tile([P, T], U8, name="tab_sc", align_bytes=64)
-        w4_sc_raw = keep.tile([P, H_PASSES, N], U8, name="w4_sc_raw", align_bytes=64)
-        nc.vector.memset(tab_sc[:].bitcast(I32), 0)
-        nc.vector.memset(w4_sc_raw[:].bitcast(I32), 0)
-        ident = keep.tile([P, P], F32, name="ident")
-        make_identity(nc, ident[:])
-
         def load_tab_scales():
-            for q in range(QUADS):
+            for quad in range(QUADS):
                 nc.sync.dma_start(
-                    tab_sc[32 * q : 32 * q + 4 * K_PASSES, :].bitcast(I32),
-                    tab_scales[:, 4 * q : 4 * q + 4, :].bitcast(I32),
+                    tab_sc[32 * quad : 32 * quad + SCALE_ROWS * K_PASSES, :].bitcast(I32),
+                    tab_scales[:, SCALE_ROWS * quad : SCALE_ROWS * (quad + 1), :].bitcast(I32),
                 )
 
         def load_w4_scales():
-            for q in range(QUADS):
+            for quad in range(QUADS):
+                rows = w4_scales[:, SCALE_ROWS * quad : SCALE_ROWS * (quad + 1), :]
                 nc.sync.dma_start(
-                    w4_sc_raw[32 * q : 32 * q + 4, :, :].bitcast(I32),
-                    w4_scales[:, 4 * q : 4 * q + 4, :].rearrange("a r n -> r a n").bitcast(I32),
+                    w4_sc_raw[32 * quad : 32 * quad + SCALE_ROWS, :, :].bitcast(I32),
+                    rows.rearrange("a r n -> r a n").bitcast(I32),
                 )
 
+        w1_raw, tab, pages = {}, {}, {}
+
         def load_w1(a, b):
-            tile = keep.tile([P, PACK, GROUP], F32, name=f"w1_raw{a}{b}", tag="w1_raw", bufs=K_PASSES)
+            w1_raw[a, b] = keep.tile([P, PACK, GROUP], F32, name=f"w1_raw{a}{b}", tag="w1_raw", bufs=K_PASSES)
             rows = w1[a * GROUP : (a + 1) * GROUP, b * GROUP : (b + 1) * GROUP]
-            nc.sync.dma_start(tile[:], rows.rearrange("(p j) c -> p j c", j=PACK))
-            return tile
+            nc.sync.dma_start(w1_raw[a, b][:], rows.rearrange("(p j) c -> p j c", j=PACK))
 
         def load_tab(a):
-            tile = keep.tile([P, T], I32, name=f"tab{a}")
-            nc.sync.dma_start(tile[:], tab_words[a].rearrange("p n i -> p (n i)").bitcast(I32))
-            return tile
+            tab[a] = keep.tile([P, T], I32, name=f"tab{a}")
+            nc.sync.dma_start(tab[a][:], tab_words[a].rearrange("p n i -> p (n i)").bitcast(I32))
 
         def dealt_rows(source, t):
             b, i = divmod(t, PACK)
             return source[b * GROUP : (b + 1) * GROUP, :].rearrange("(p i) c -> p i c", i=PACK)[:, i, :]
 
-        pages = {}
         gm_sb = keep.tile([P, TILES, PICKS], F32, name="gm_sb")
 
         def load_page(t):
@@ -99,35 +104,34 @@ def tile_list_motion_cue_features_kernel(
         def load_gm(t):
             nc.sync.dma_start(gm_sb[:, t, :], dealt_rows(gm, t))
 
-        w1_raw, tab = {}, {}
-        w1_raw[0, 0] = load_w1(0, 0)
+        load_w1(0, 0)
         idx = load_list(offs, "idx")
         wgs_sb = keep.tile([P, S], F32, name="wgs_sb")
         nc.sync.dma_start(wgs_sb[:], wgs)
         gain_sb = load_vector(gain, "gain_sb")
-        tab[0] = load_tab(0)
-        w1_raw[1, 0] = load_w1(1, 0)
+        load_tab(0)
+        load_w1(1, 0)
         b1_sb = load_vector(b1, "b1_sb")
         idx2 = load_list(offs2, "idx2")
         load_tab_scales()
-        tab[1] = load_tab(1)
-        w1_raw[2, 0] = load_w1(2, 0)
+        load_tab(1)
+        load_w1(2, 0)
         load_w4_scales()
-        tab[2] = load_tab(2)
+        load_tab(2)
         w4_raw = keep.tile([P, H_PASSES, 2 * N], U8, name="w4_raw", align_bytes=64)
         nc.sync.dma_start(w4_raw[:].bitcast(I32), w4_words.rearrange("a p n -> p a n").bitcast(I32))
         load_page(0)
         idx3 = load_list(offs3, "idx3")
         gv_sb = load_vector(gv, "gv_sb")
         load_page(1)
+        load_w1(0, 1)
         wgt_sb = keep.tile([P, PICKS], F32, name="wgt_sb")
         nc.sync.dma_start(wgt_sb[:], wgt)
-        load_gm(0)
-        w1_raw[0, 1] = load_w1(0, 1)
-        w1_raw[1, 1] = load_w1(1, 1)
+        load_w1(1, 1)
         load_page(2)
+        load_gm(0)
         load_gm(1)
-        w1_raw[2, 1] = load_w1(2, 1)
+        load_w1(2, 1)
         for t in range(3, TILES):
             load_page(t)
             load_gm(t - 1)
@@ -138,7 +142,7 @@ def tile_list_motion_cue_features_kernel(
             nc.tensor.transpose(wgs_t_ps[:, c, :], wgs_sb[:, c * P : (c + 1) * P], ident[:])
         wgs_t = keep.tile([P, S // P, PACK, QUADS, 32], F32, name="wgs_t")
         nc.scalar.copy(
-            wgs_t[:].rearrange("j c i r p -> j c r p i"),
+            wgs_t[:].rearrange("j c i quad p -> j c quad p i"),
             wgs_t_ps[:].rearrange("j c (p i) -> j c p i", i=PACK).unsqueeze(2).broadcast_to([P, S // P, QUADS, 32, PACK]),
         )
         wz = keep.tile([P, TILES + 2, S], F32, name="wz")
@@ -146,36 +150,34 @@ def tile_list_motion_cue_features_kernel(
         for i in range(PACK):
             bank = aux_psum.tile([P, S], F32, name=f"dealt{i}", tag="aux")
             for c in range(S // P):
-                nc.tensor.transpose(bank[:, c * P : (c + 1) * P], wgs_t[:, c, i, :, :].rearrange("j r p -> j (r p)"), ident[:])
+                turned = wgs_t[:, c, i, :, :].rearrange("j quad p -> j (quad p)")
+                nc.tensor.transpose(bank[:, c * P : (c + 1) * P], turned, ident[:])
             dealt_ps.append(bank)
 
         def scale_wgs(t):
             nc.scalar.activation(wz[:, t, :], dealt_ps[t % PACK][:], ACT.Copy, scale=column(gain_sb, t))
 
-        w1_codes, w1_sc = {}, {}
+        w1_codes, w1_sc, v_codes, h_banks = {}, {}, {}, {}
 
         def quantize_w1(a, b, shares):
             grouped = ring.tile([P, PACK, P, PACK], BF16, name="w1_bf", align_bytes=64)
-            for cast, m0, m1 in shares:
+            for cast, first, end in shares:
                 cast(
-                    grouped[:].rearrange("p t m j -> p m j t")[:, m0:m1],
-                    w1_raw[a, b][:].rearrange("p j (m t) -> p m j t", t=PACK)[:, m0:m1],
+                    grouped[:].rearrange("p i m j -> p m j i")[:, first:end],
+                    w1_raw[a, b][:].rearrange("p j (m i) -> p m j i", i=PACK)[:, first:end],
                 )
             w1_codes[a, b] = keep.tile([P, GROUP], U32, name=f"w1_codes{a}{b}", align_bytes=64)
             w1_sc[a, b] = keep.tile([P, GROUP], U8, name=f"w1_sc{a}{b}", align_bytes=64)
             nc.vector.quantize_mx(
                 out=w1_codes[a, b][:].bitcast(FP8X4), scales=w1_sc[a, b][:],
-                in_=grouped[:].rearrange("p t m j -> p (t m j)"),
+                in_=grouped[:].rearrange("p i m j -> p (i m j)"),
             )
-
-        v_codes = {}
 
         def gather_tab(a):
             v_codes[a] = keep.tile([P, S], U32, name=f"v_codes{a}", align_bytes=64)
             nc.vector.tensor_copy(v_codes[a][:], tab[a][:].bitcast(U32).indirect(idx[:]))
 
         v_sc = keep.tile([P, S], U8, name="v_sc", align_bytes=64)
-        h_banks = {}
 
         def first_pass(a, b):
             for i in range(PACK):
@@ -186,7 +188,7 @@ def tile_list_motion_cue_features_kernel(
                 nc.tensor.matmul_mx(
                     out=h_banks[t][:],
                     lhsT=w1_codes[a, b][:, cols].bitcast(FP8X4), lhsT_scale=w1_sc[a, b][:, cols],
-                    rhs=v_codes[a][:].bitcast(FP8X4), rhs_scale=v_sc[4 * a :, :],
+                    rhs=v_codes[a][:].bitcast(FP8X4), rhs_scale=v_sc[SCALE_ROWS * a :, :],
                     start=(a == 0), stop=(a == K_PASSES - 1),
                 )
 
@@ -195,30 +197,30 @@ def tile_list_motion_cue_features_kernel(
         def tanh(t):
             nc.scalar.activation(hx[:, t, :], h_banks[t][:], ACT.Tanh, bias=column(b1_sb, t))
 
-        quantize_w1(0, 0, [(nc.scalar.copy, 0, P)])
+        on_scalar = [(nc.scalar.copy, 0, P)]
+        quantize_w1(0, 0, on_scalar)
         gather_tab(0)
         nc.vector.tensor_copy(v_sc[:], tab_sc[:].indirect(idx[:]))
         first_pass(0, 0)
         scale_wgs(0)
-        quantize_w1(1, 0, [(nc.scalar.copy, 0, P)])
+        quantize_w1(1, 0, on_scalar)
         gather_tab(1)
         first_pass(1, 0)
         scale_wgs(1)
+        quantize_w1(2, 0, [(nc.vector.tensor_copy, 0, VECTOR_SHARE), (nc.scalar.copy, VECTOR_SHARE, P)])
 
-        quantize_w1(2, 0, [(nc.vector.tensor_copy, 0, 80), (nc.scalar.copy, 80, P)])
         w4_sc = keep.tile([P, H_PASSES, PACK, P], U8, name="w4_sc", align_bytes=64)
         nc.vector.tensor_copy(
-            w4_sc[:].rearrange("p a t m -> p a m t"),
-            w4_sc_raw[:].rearrange("p a (m t) -> p a m t", t=PACK),
+            w4_sc[:].rearrange("p b i m -> p b m i"),
+            w4_sc_raw[:].rearrange("p b (m i) -> p b m i", i=PACK),
         )
         gather_tab(2)
         first_pass(2, 0)
         w4_codes = keep.tile([P, H_PASSES, PACK, 2 * P], U8, name="w4_codes", align_bytes=64)
         nc.vector.tensor_copy(
-            w4_codes[:].bitcast(U16).rearrange("p a t m -> p a m t"),
-            w4_raw[:].bitcast(U16).rearrange("p a (m t) -> p a m t", t=PACK),
+            w4_codes[:].bitcast(U16).rearrange("p b i m -> p b m i"),
+            w4_raw[:].bitcast(U16).rearrange("p b (m i) -> p b m i", i=PACK),
         )
-
         for t in range(PACK):
             tanh(t)
         for t in range(2, TILES):
@@ -231,27 +233,26 @@ def tile_list_motion_cue_features_kernel(
             return w1_raw[t, 1][:, 0, :] if t < K_PASSES else hx[:, t + 1, :]
 
         def gather(t, m0, m1):
-            nc.vector.tensor_tensor(
-                picked(t)[:, m0:m1], pages[t][:].indirect(idx3[:, m0 // 16 : m1 // 16]), wgt_sb[:, m0:m1], ALU.mult
-            )
+            cells = pages[t][:].indirect(idx3[:, m0 // LIST : m1 // LIST])
+            nc.vector.tensor_tensor(picked(t)[:, m0:m1], cells, wgt_sb[:, m0:m1], ALU.mult)
 
-        def modulate(x, factors):
-            product = ring.tile(list(x.shape), F32, name="product", bufs=3)
-            nc.vector.tensor_tensor(product[:], x, factors, ALU.mult)
+        def modulate(t, m0, m1):
+            product = ring.tile([P, m1 - m0], F32, name="product", bufs=3)
+            nc.vector.tensor_tensor(product[:], picked(t)[:, m0:m1], gm_sb[:, t, m0:m1], ALU.mult)
             return product
 
         def larger(t, product, m0, m1):
             nc.vector.scalar_tensor_tensor(
-                wz[:, t + 2, m0:m1], picked(t)[:, m0:m1], column(gv_sb, t), product, ALU.add, ALU.max
+                wz[:, t + 2, m0:m1], picked(t)[:, m0:m1], column(gv_sb, t), product[:], ALU.add, ALU.max
             )
+
+        def interleave(cast, grouped, slices):
+            cast(grouped.rearrange("p (c e) i -> p c i e", e=RUN), slices.rearrange("p i (c e) -> p c i e", e=RUN))
 
         def quantize_z(b, m0, m1, cast):
             width = m1 - m0
             grouped = keep.tile([P, width, PACK], BF16, name=f"z_bf{b}_{m0}", align_bytes=64)
-            cast(
-                grouped[:].rearrange("p (c e) i -> p c i e", e=4),
-                wz[:, PACK * b + 2 : PACK * b + 6, m0:m1].rearrange("p i (c e) -> p c i e", e=4),
-            )
+            interleave(cast, grouped[:], wz[:, PACK * b + 2 : PACK * (b + 1) + 2, m0:m1])
             codes = keep.tile([P, width], U32, name=f"z_codes{b}_{m0}", align_bytes=64)
             scales = keep.tile([P, width], U8, name=f"z_sc{b}_{m0}", align_bytes=64)
             nc.vector.quantize_mx(out=codes[:].bitcast(FP8X4), scales=scales[:], in_=grouped[:].rearrange("p m i -> p (m i)"))
@@ -261,31 +262,29 @@ def tile_list_motion_cue_features_kernel(
 
         def second_pass(b, q, codes, scales):
             per_bank = 2 if q == CHUNKS - 1 else PACK
-            for t in range(PACK):
-                first, place = t - t % per_bank, t % per_bank
+            for i in range(PACK):
+                first, place = i - i % per_bank, i % per_bank
                 if b == 0 and place == 0:
                     pool, tag = (h_psum, "h") if per_bank < PACK else (aux_psum, "aux")
                     y_banks[q, first] = pool.tile([P, per_bank, CHUNK], F32, name=f"y{q}_{first}", tag=tag)
                 nc.tensor.matmul_mx(
                     out=y_banks[q, first][:, place, :],
-                    lhsT=w4_codes[:, b, t, :].bitcast(FP4X4),
-                    lhsT_scale=w4_sc[:, b, t, :],
+                    lhsT=w4_codes[:, b, i, :].bitcast(FP4X4), lhsT_scale=w4_sc[:, b, i, :],
                     rhs=codes.bitcast(FP8X4), rhs_scale=scales,
                     start=(b == 0 and place == 0), stop=(b == H_PASSES - 1 and place == per_bank - 1),
                 )
 
-        products = {}
         scatter(0)
         for t in range(TILES - 1):
             scatter(t + 1)
             if t >= 1:
-                products[t - 1] = modulate(picked(t - 1), gm_sb[:, t - 1, :])
+                product = modulate(t - 1, 0, PICKS)
             if t < K_PASSES:
-                quantize_w1(t, 1, [(nc.scalar.copy, 0, P)])
+                quantize_w1(t, 1, on_scalar)
                 first_pass(t, 1)
             gather(t, 0, PICKS)
             if t >= 1:
-                larger(t - 1, products[t - 1][:], 0, PICKS)
+                larger(t - 1, product, 0, PICKS)
             if t == K_PASSES - 1:
                 for later in range(PACK, TILES):
                     tanh(later)
@@ -295,42 +294,41 @@ def tile_list_motion_cue_features_kernel(
                     cols = slice(q * CHUNK, (q + 1) * CHUNK)
                     second_pass(0, q, codes[:, cols], scales[:, cols])
 
-        y_rows = out_0.rearrange("(p t) m -> p t m", t=PACK)
-        y_words = out_1[0].rearrange("p m t -> p (m t)").bitcast(I32)
+        y_rows = out_0.rearrange("(p i) m -> p i m", i=PACK)
+        y_words = out_1[0].rearrange("p m i -> p (m i)").bitcast(I32)
         y_codes = keep.tile([P, PICKS], U32, name="y_codes", align_bytes=64)
         y_sc = keep.tile([P, PICKS], U8, name="y_sc", align_bytes=64)
+        before_last = {0: CHUNK, 1: PICKS}
         for q in range(CHUNKS):
             m0, m1 = q * CHUNK, (q + 1) * CHUNK
             last = q == CHUNKS - 1
             gather(TILES - 1, m0, m1)
-            if q < 2:
-                upto = m1 if q == 0 else PICKS
-                product = modulate(picked(TILES - 2)[:, m0:upto], gm_sb[:, TILES - 2, m0:upto])
-                larger(TILES - 2, product[:], m0, upto)
-            product = modulate(picked(TILES - 1)[:, m0:m1], gm_sb[:, TILES - 1, m0:m1])
-            larger(TILES - 1, product[:], m0, m1)
+            if q in before_last:
+                larger(TILES - 2, modulate(TILES - 2, m0, before_last[q]), m0, before_last[q])
+            larger(TILES - 1, modulate(TILES - 1, m0, m1), m0, m1)
             codes, scales = quantize_z(1, m0, m1, nc.scalar.copy if q == 0 else nc.vector.tensor_copy)
             second_pass(1, q, codes[:], scales[:])
             y_bf = keep.tile([P, CHUNK, PACK], BF16, name=f"y_bf{q}", align_bytes=64)
             y_sb = keep.tile([P, PACK, CHUNK], F32, name=f"y_sb{q}")
             if q == 0:
-                nc.scalar.copy(y_bf[:], y_banks[q, 0][:].rearrange("p t m -> p m t"))
+                nc.scalar.copy(y_bf[:], y_banks[q, 0][:].rearrange("p i m -> p m i"))
             if last:
                 nc.scalar.copy(y_sb[:, 0:2, :], y_banks[q, 0][:])
                 nc.vector.tensor_copy(y_sb[:, 2:4, :], y_banks[q, 2][:])
             else:
                 nc.scalar.copy(y_sb[:], y_banks[q, 0][:])
             if q > 0:
-                nc.vector.tensor_copy(
-                    y_bf[:].rearrange("p (c e) t -> p c t e", e=4), y_sb[:].rearrange("p t (c e) -> p c t e", e=4)
-                )
+                interleave(nc.vector.tensor_copy, y_bf[:], y_sb[:])
             nc.vector.quantize_mx(
-                out=y_codes[:, m0:m1].bitcast(FP8X4), scales=y_sc[:, m0:m1], in_=y_bf[:].rearrange("p m t -> p (m t)")
+                out=y_codes[:, m0:m1].bitcast(FP8X4), scales=y_sc[:, m0:m1], in_=y_bf[:].rearrange("p m i -> p (m i)")
             )
             (nc.scalar if last else nc.sync).dma_start(y_rows[:, :, m0:m1], y_sb[:])
             if q >= CHUNKS - 2:
                 stored = m0 if last else 0
                 nc.sync.dma_start(y_words[:, stored:m1], y_codes[:, stored:m1].bitcast(I32))
-        for q in range(QUADS):
-            queue = nc.sync if q < 2 else nc.scalar
-            queue.dma_start(out_2[0, 4 * q : 4 * q + 4, :].bitcast(I32), y_sc[32 * q : 32 * q + 4, :].bitcast(I32))
+        for quad in range(QUADS):
+            queue = nc.sync if quad < QUADS // 2 else nc.scalar
+            queue.dma_start(
+                out_2[0, SCALE_ROWS * quad : SCALE_ROWS * (quad + 1), :].bitcast(I32),
+                y_sc[32 * quad : 32 * quad + SCALE_ROWS, :].bitcast(I32),
+            )

from contextlib import ExitStack

import concourse.mybir as mybir
from concourse.masks import make_identity

K, T, H, S, T2, PICKS, N = 1536, 2048, 1024, 512, 1024, 512, 512
FLOPS = 2 * K * H * S + 2 * H * N * PICKS

F32 = mybir.dt.float32
BF16 = mybir.dt.bfloat16
I32 = mybir.dt.int32
U32 = mybir.dt.uint32
U16 = mybir.dt.uint16
U8 = mybir.dt.uint8
FP8X4 = mybir.dt.float8_e4m3fn_x4
FP4X4 = mybir.dt.float4_e2m1fn_x4
ALU = mybir.AluOpType
ACT = mybir.ActivationFunctionType

P = 128
PACK = 4
GROUP = P * PACK
K_PASSES = K // GROUP
H_PASSES = H // GROUP
TILES = H // P
LIST = 16
QUADS = 4
SCALE_ROWS = 4
RUN = 4
CHUNK = 128
CHUNKS = PICKS // CHUNK
VECTOR_SHARE = 80
H_BANKS, AUX_BANKS = 4, 4


def tile_list_motion_cue_features_kernel(
    tc, tab_words, tab_scales, offs, w1, b1, gain, page0, wgs, offs2, wgt, offs3, gm, gv,
    w4_words, w4_scales, out_0, out_1, out_2,
):
    nc = tc.nc
    with ExitStack() as ctx:
        lists = ctx.enter_context(tc.tile_pool(name="lists", bufs=1))
        keep = ctx.enter_context(tc.tile_pool(name="keep", bufs=1))
        ring = ctx.enter_context(tc.tile_pool(name="ring", bufs=2))
        h_psum = ctx.enter_context(tc.psum_pool(name="h_psum", bufs=H_BANKS))
        aux_psum = ctx.enter_context(tc.psum_pool(name="aux_psum", bufs=AUX_BANKS))

        tab_sc = keep.tile([P, T], U8, name="tab_sc", align_bytes=64)
        w4_sc_raw = keep.tile([P, H_PASSES, N], U8, name="w4_sc_raw", align_bytes=64)
        nc.vector.memset(tab_sc[:].bitcast(I32), 0)
        nc.vector.memset(w4_sc_raw[:].bitcast(I32), 0)
        ident = keep.tile([P, P], F32, name="ident")
        make_identity(nc, ident[:])

        def load_list(source, name):
            tile = lists.tile([P, S // LIST], U16, name=name)
            nc.sync.dma_start(tile[:], source)
            return tile

        def load_vector(source, name):
            tile = keep.tile([P, H_PASSES, PACK], F32, name=name)
            nc.sync.dma_start(tile[:], source.rearrange("(b p i) -> p b i", b=H_PASSES, i=PACK))
            return tile

        def column(vector, t):
            return vector[:, t // PACK, t % PACK : t % PACK + 1]

        def load_tab_scales():
            for quad in range(QUADS):
                nc.sync.dma_start(
                    tab_sc[32 * quad : 32 * quad + SCALE_ROWS * K_PASSES, :].bitcast(I32),
                    tab_scales[:, SCALE_ROWS * quad : SCALE_ROWS * (quad + 1), :].bitcast(I32),
                )

        def load_w4_scales():
            for quad in range(QUADS):
                rows = w4_scales[:, SCALE_ROWS * quad : SCALE_ROWS * (quad + 1), :]
                nc.sync.dma_start(
                    w4_sc_raw[32 * quad : 32 * quad + SCALE_ROWS, :, :].bitcast(I32),
                    rows.rearrange("a r n -> r a n").bitcast(I32),
                )

        w1_raw, tab, pages = {}, {}, {}

        def load_w1(a, b):
            w1_raw[a, b] = keep.tile([P, PACK, GROUP], F32, name=f"w1_raw{a}{b}", tag="w1_raw", bufs=K_PASSES)
            rows = w1[a * GROUP : (a + 1) * GROUP, b * GROUP : (b + 1) * GROUP]
            nc.sync.dma_start(w1_raw[a, b][:], rows.rearrange("(p j) c -> p j c", j=PACK))

        def load_tab(a):
            tab[a] = keep.tile([P, T], I32, name=f"tab{a}")
            nc.sync.dma_start(tab[a][:], tab_words[a].rearrange("p n i -> p (n i)").bitcast(I32))

        def dealt_rows(source, t):
            b, i = divmod(t, PACK)
            return source[b * GROUP : (b + 1) * GROUP, :].rearrange("(p i) c -> p i c", i=PACK)[:, i, :]

        gm_sb = keep.tile([P, TILES, PICKS], F32, name="gm_sb")

        def load_page(t):
            pages[t] = keep.tile([P, T2], F32, name=f"page{t}")
            nc.sync.dma_start(pages[t][:], dealt_rows(page0, t))

        def load_gm(t):
            nc.sync.dma_start(gm_sb[:, t, :], dealt_rows(gm, t))

        load_w1(0, 0)
        idx = load_list(offs, "idx")
        wgs_sb = keep.tile([P, S], F32, name="wgs_sb")
        nc.sync.dma_start(wgs_sb[:], wgs)
        gain_sb = load_vector(gain, "gain_sb")
        load_tab(0)
        load_w1(1, 0)
        b1_sb = load_vector(b1, "b1_sb")
        idx2 = load_list(offs2, "idx2")
        load_tab_scales()
        load_tab(1)
        load_w1(2, 0)
        load_w4_scales()
        load_tab(2)
        w4_raw = keep.tile([P, H_PASSES, 2 * N], U8, name="w4_raw", align_bytes=64)
        nc.sync.dma_start(w4_raw[:].bitcast(I32), w4_words.rearrange("a p n -> p a n").bitcast(I32))
        load_page(0)
        idx3 = load_list(offs3, "idx3")
        gv_sb = load_vector(gv, "gv_sb")
        load_page(1)
        load_w1(0, 1)
        wgt_sb = keep.tile([P, PICKS], F32, name="wgt_sb")
        nc.sync.dma_start(wgt_sb[:], wgt)
        load_w1(1, 1)
        load_page(2)
        load_gm(0)
        load_gm(1)
        load_w1(2, 1)
        for t in range(3, TILES):
            load_page(t)
            load_gm(t - 1)
        load_gm(TILES - 1)

        wgs_t_ps = aux_psum.tile([P, S // P, P], F32, name="wgs_t_ps", tag="aux")
        for c in range(S // P):
            nc.tensor.transpose(wgs_t_ps[:, c, :], wgs_sb[:, c * P : (c + 1) * P], ident[:])
        wgs_t = keep.tile([P, S // P, PACK, QUADS, 32], F32, name="wgs_t")
        nc.scalar.copy(
            wgs_t[:].rearrange("j c i quad p -> j c quad p i"),
            wgs_t_ps[:].rearrange("j c (p i) -> j c p i", i=PACK).unsqueeze(2).broadcast_to([P, S // P, QUADS, 32, PACK]),
        )
        wz = keep.tile([P, TILES + 2, S], F32, name="wz")
        dealt_ps = []
        for i in range(PACK):
            bank = aux_psum.tile([P, S], F32, name=f"dealt{i}", tag="aux")
            for c in range(S // P):
                turned = wgs_t[:, c, i, :, :].rearrange("j quad p -> j (quad p)")
                nc.tensor.transpose(bank[:, c * P : (c + 1) * P], turned, ident[:])
            dealt_ps.append(bank)

        def scale_wgs(t):
            nc.scalar.activation(wz[:, t, :], dealt_ps[t % PACK][:], ACT.Copy, scale=column(gain_sb, t))

        w1_codes, w1_sc, v_codes, h_banks = {}, {}, {}, {}

        def quantize_w1(a, b, shares):
            grouped = ring.tile([P, PACK, P, PACK], BF16, name="w1_bf", align_bytes=64)
            for cast, first, end in shares:
                cast(
                    grouped[:].rearrange("p i m j -> p m j i")[:, first:end],
                    w1_raw[a, b][:].rearrange("p j (m i) -> p m j i", i=PACK)[:, first:end],
                )
            w1_codes[a, b] = keep.tile([P, GROUP], U32, name=f"w1_codes{a}{b}", align_bytes=64)
            w1_sc[a, b] = keep.tile([P, GROUP], U8, name=f"w1_sc{a}{b}", align_bytes=64)
            nc.vector.quantize_mx(
                out=w1_codes[a, b][:].bitcast(FP8X4), scales=w1_sc[a, b][:],
                in_=grouped[:].rearrange("p i m j -> p (i m j)"),
            )

        def gather_tab(a):
            v_codes[a] = keep.tile([P, S], U32, name=f"v_codes{a}", align_bytes=64)
            nc.vector.tensor_copy(v_codes[a][:], tab[a][:].bitcast(U32).indirect(idx[:]))

        v_sc = keep.tile([P, S], U8, name="v_sc", align_bytes=64)

        def first_pass(a, b):
            for i in range(PACK):
                t = PACK * b + i
                if a == 0:
                    h_banks[t] = h_psum.tile([P, S], F32, name=f"h{t}", tag="h")
                cols = slice(i * P, (i + 1) * P)
                nc.tensor.matmul_mx(
                    out=h_banks[t][:],
                    lhsT=w1_codes[a, b][:, cols].bitcast(FP8X4), lhsT_scale=w1_sc[a, b][:, cols],
                    rhs=v_codes[a][:].bitcast(FP8X4), rhs_scale=v_sc[SCALE_ROWS * a :, :],
                    start=(a == 0), stop=(a == K_PASSES - 1),
                )

        hx = keep.tile([P, TILES + 1, S], F32, name="hx")

        def tanh(t):
            nc.scalar.activation(hx[:, t, :], h_banks[t][:], ACT.Tanh, bias=column(b1_sb, t))

        on_scalar = [(nc.scalar.copy, 0, P)]
        quantize_w1(0, 0, on_scalar)
        gather_tab(0)
        nc.vector.tensor_copy(v_sc[:], tab_sc[:].indirect(idx[:]))
        first_pass(0, 0)
        scale_wgs(0)
        quantize_w1(1, 0, on_scalar)
        gather_tab(1)
        first_pass(1, 0)
        scale_wgs(1)
        quantize_w1(2, 0, [(nc.vector.tensor_copy, 0, VECTOR_SHARE), (nc.scalar.copy, VECTOR_SHARE, P)])

        w4_sc = keep.tile([P, H_PASSES, PACK, P], U8, name="w4_sc", align_bytes=64)
        nc.vector.tensor_copy(
            w4_sc[:].rearrange("p b i m -> p b m i"),
            w4_sc_raw[:].rearrange("p b (m i) -> p b m i", i=PACK),
        )
        gather_tab(2)
        first_pass(2, 0)
        w4_codes = keep.tile([P, H_PASSES, PACK, 2 * P], U8, name="w4_codes", align_bytes=64)
        nc.vector.tensor_copy(
            w4_codes[:].bitcast(U16).rearrange("p b i m -> p b m i"),
            w4_raw[:].bitcast(U16).rearrange("p b (m i) -> p b m i", i=PACK),
        )
        for t in range(PACK):
            tanh(t)
        for t in range(2, TILES):
            scale_wgs(t)

        def scatter(t):
            nc.vector.tensor_tensor(pages[t][:].indirect(idx2[:]), hx[:, t, :], wz[:, t, :], ALU.mult)

        def picked(t):
            return w1_raw[t, 1][:, 0, :] if t < K_PASSES else hx[:, t + 1, :]

        def gather(t, m0, m1):
            cells = pages[t][:].indirect(idx3[:, m0 // LIST : m1 // LIST])
            nc.vector.tensor_tensor(picked(t)[:, m0:m1], cells, wgt_sb[:, m0:m1], ALU.mult)

        def modulate(t, m0, m1):
            product = ring.tile([P, m1 - m0], F32, name="product", bufs=3)
            nc.vector.tensor_tensor(product[:], picked(t)[:, m0:m1], gm_sb[:, t, m0:m1], ALU.mult)
            return product

        def larger(t, product, m0, m1):
            nc.vector.scalar_tensor_tensor(
                wz[:, t + 2, m0:m1], picked(t)[:, m0:m1], column(gv_sb, t), product[:], ALU.add, ALU.max
            )

        def interleave(cast, grouped, slices):
            cast(grouped.rearrange("p (c e) i -> p c i e", e=RUN), slices.rearrange("p i (c e) -> p c i e", e=RUN))

        def quantize_z(b, m0, m1, cast):
            width = m1 - m0
            grouped = keep.tile([P, width, PACK], BF16, name=f"z_bf{b}_{m0}", align_bytes=64)
            interleave(cast, grouped[:], wz[:, PACK * b + 2 : PACK * (b + 1) + 2, m0:m1])
            codes = keep.tile([P, width], U32, name=f"z_codes{b}_{m0}", align_bytes=64)
            scales = keep.tile([P, width], U8, name=f"z_sc{b}_{m0}", align_bytes=64)
            nc.vector.quantize_mx(out=codes[:].bitcast(FP8X4), scales=scales[:], in_=grouped[:].rearrange("p m i -> p (m i)"))
            return codes, scales

        y_banks = {}

        def second_pass(b, q, codes, scales):
            per_bank = 2 if q == CHUNKS - 1 else PACK
            for i in range(PACK):
                first, place = i - i % per_bank, i % per_bank
                if b == 0 and place == 0:
                    pool, tag = (h_psum, "h") if per_bank < PACK else (aux_psum, "aux")
                    y_banks[q, first] = pool.tile([P, per_bank, CHUNK], F32, name=f"y{q}_{first}", tag=tag)
                nc.tensor.matmul_mx(
                    out=y_banks[q, first][:, place, :],
                    lhsT=w4_codes[:, b, i, :].bitcast(FP4X4), lhsT_scale=w4_sc[:, b, i, :],
                    rhs=codes.bitcast(FP8X4), rhs_scale=scales,
                    start=(b == 0 and place == 0), stop=(b == H_PASSES - 1 and place == per_bank - 1),
                )

        scatter(0)
        for t in range(TILES - 1):
            scatter(t + 1)
            if t >= 1:
                product = modulate(t - 1, 0, PICKS)
            if t < K_PASSES:
                quantize_w1(t, 1, on_scalar)
                first_pass(t, 1)
            gather(t, 0, PICKS)
            if t >= 1:
                larger(t - 1, product, 0, PICKS)
            if t == K_PASSES - 1:
                for later in range(PACK, TILES):
                    tanh(later)
            if t == PACK:
                codes, scales = quantize_z(0, 0, PICKS, nc.scalar.copy)
                for q in range(CHUNKS):
                    cols = slice(q * CHUNK, (q + 1) * CHUNK)
                    second_pass(0, q, codes[:, cols], scales[:, cols])

        y_rows = out_0.rearrange("(p i) m -> p i m", i=PACK)
        y_words = out_1[0].rearrange("p m i -> p (m i)").bitcast(I32)
        y_codes = keep.tile([P, PICKS], U32, name="y_codes", align_bytes=64)
        y_sc = keep.tile([P, PICKS], U8, name="y_sc", align_bytes=64)
        before_last = {0: CHUNK, 1: PICKS}
        for q in range(CHUNKS):
            m0, m1 = q * CHUNK, (q + 1) * CHUNK
            last = q == CHUNKS - 1
            gather(TILES - 1, m0, m1)
            if q in before_last:
                larger(TILES - 2, modulate(TILES - 2, m0, before_last[q]), m0, before_last[q])
            larger(TILES - 1, modulate(TILES - 1, m0, m1), m0, m1)
            codes, scales = quantize_z(1, m0, m1, nc.scalar.copy if q == 0 else nc.vector.tensor_copy)
            second_pass(1, q, codes[:], scales[:])
            y_bf = keep.tile([P, CHUNK, PACK], BF16, name=f"y_bf{q}", align_bytes=64)
            y_sb = keep.tile([P, PACK, CHUNK], F32, name=f"y_sb{q}")
            if q == 0:
                nc.scalar.copy(y_bf[:], y_banks[q, 0][:].rearrange("p i m -> p m i"))
            if last:
                nc.scalar.copy(y_sb[:, 0:2, :], y_banks[q, 0][:])
                nc.vector.tensor_copy(y_sb[:, 2:4, :], y_banks[q, 2][:])
            else:
                nc.scalar.copy(y_sb[:], y_banks[q, 0][:])
            if q > 0:
                interleave(nc.vector.tensor_copy, y_bf[:], y_sb[:])
            nc.vector.quantize_mx(
                out=y_codes[:, m0:m1].bitcast(FP8X4), scales=y_sc[:, m0:m1], in_=y_bf[:].rearrange("p m i -> p (m i)")
            )
            (nc.scalar if last else nc.sync).dma_start(y_rows[:, :, m0:m1], y_sb[:])
            if q >= CHUNKS - 2:
                stored = m0 if last else 0
                nc.sync.dma_start(y_words[:, stored:m1], y_codes[:, stored:m1].bitcast(I32))
        for quad in range(QUADS):
            queue = nc.sync if quad < QUADS // 2 else nc.scalar
            queue.dma_start(
                out_2[0, SCALE_ROWS * quad : SCALE_ROWS * (quad + 1), :].bitcast(I32),
                y_sc[32 * quad : 32 * quad + SCALE_ROWS, :].bitcast(I32),
            )
